import numpy as np
import ml_dtypes


def mxq(x, axis, fmt="e4m3"):
    dtype, down = {"e4m3": (ml_dtypes.float8_e4m3fn, 7), "e5m2": (ml_dtypes.float8_e5m2, 14)}[fmt]
    v = np.moveaxis(np.asarray(x, np.float32).astype(ml_dtypes.bfloat16).astype(np.float64), axis, -1)
    blocks = v.reshape(v.shape[:-1] + (-1, 32))
    amax = np.abs(blocks).max(-1, keepdims=True)
    byte = np.maximum(np.where(amax > 0, np.frexp(amax)[1] - 1 + 127, 0) - down, 1)
    scale = np.exp2(byte - 127.0)
    codes = (blocks / scale).astype(np.float32).astype(dtype).astype(np.float64)
    return np.moveaxis((codes * scale).reshape(v.shape), -1, axis)


WIDE = False


def mx_kscale(k):
    if not WIDE:
        return np.ones(k)
    levels = np.array([10, -10, 5, -5, 0])
    if k % 512:
        return np.exp2(np.random.permutation(np.resize(levels, k // 32))).repeat(32)
    a = np.empty((k // 512, 16))
    for p in range(k // 512):
        a[p, :8] = np.random.permutation(np.resize(levels, 8))
        for g in range(8):
            far = levels[np.abs(levels - a[p, g]) >= 10]
            a[p, g + 8] = far[np.random.randint(len(far))]
    return np.exp2(a.ravel()).repeat(32)


def f64(x):
    return np.asarray(x).astype(np.float64)


def striped(idx):
    return np.tile(np.asarray(idx).reshape(-1, 16).T, (8, 1)).astype(np.uint16)


def unstriped(offs):
    return offs[:16].T.reshape(-1).astype(np.int64)


E2M1 = np.array([0.0, 0.5, 1.0, 1.5, 2.0, 3.0, 4.0, 6.0, -0.0, -0.5, -1.0, -1.5, -2.0, -3.0, -4.0, -6.0])


def pack_weight(w, fmt):
    k, n = w.shape
    w = f64(np.asarray(w, np.float32).astype(ml_dtypes.bfloat16)).reshape(k // 32, 32, n)
    amax = np.abs(w).max(1)
    if fmt == "e4m3":
        byte = np.frexp(amax)[1] - 1 + 127 - 7
    else:
        mant, ex = np.frexp(amax / 6.0)
        byte = np.where(mant > 0.5, ex, ex - 1) + 127
    byte = np.clip(np.where(amax > 0, byte, 1), 1, 254)
    scaled = (w * np.exp2(127.0 - byte)[:, None, :]).reshape(k, n).astype(np.float32)
    by_word = np.ascontiguousarray(scaled.reshape(k // 512, 128, 4, n).transpose(0, 1, 3, 2))
    if fmt == "e4m3":
        words = by_word.astype(ml_dtypes.float8_e4m3fn).view(np.uint8)
    else:
        c = by_word.astype(ml_dtypes.float4_e2m1fn).view(np.uint8) & 0xF
        words = (c[..., 0::2] | (c[..., 1::2] << 4)).reshape(k // 512, 128, 2 * n)
    return np.ascontiguousarray(words), np.ascontiguousarray(byte.astype(np.uint8).reshape(k // 512, 16, n))


def unpack_weight(words, scales, fmt):
    g, _, n = scales.shape
    words = np.ascontiguousarray(words).reshape(g, 128, n, -1)
    if fmt == "e4m3":
        vals = words.view(ml_dtypes.float8_e4m3fn).astype(np.float64)
    else:
        nib = np.empty((g, 128, n, 4), np.uint8)
        nib[..., 0::2] = words & 0xF
        nib[..., 1::2] = words >> 4
        vals = E2M1[nib]
    vals = vals * np.repeat(np.exp2(scales.astype(np.float64) - 127.0), 8, axis=1)[..., None]
    return vals.transpose(0, 1, 3, 2).reshape(g * 512, n)


def softplus(v):
    return np.log(1.0 + np.exp(v))


def sigmoid(v):
    return 1.0 / (1.0 + np.exp(-v))


D, E, T, I, Q = 512, 512, 2048, 512, 128


def setup_inputs():
    n = np.random.standard_normal
    idx = np.random.permutation(T)[:I]
    fd = mx_kscale(D)
    fe = mx_kscale(E)
    keysp = pack_weight(n((D, T)) / fd[:, None], "e2m1")
    valsp = pack_weight(n((E, T)) / fe[:, None], "e2m1")
    return {
        "query": (n((D, Q)) * 0.6 / np.sqrt(D) * fd[:, None]).astype(np.float32),
        "query2": (n((D, Q)) * 1.0 / np.sqrt(D) * fd[:, None]).astype(np.float32),
        "keys_words": keysp[0],
        "keys_scales": keysp[1],
        "strict": (np.random.uniform(0.4, 1.2, (Q, 1))).astype(np.float32),
        "gout": (n((E, Q)) * 1 / np.sqrt(E) * fe[:, None]).astype(np.float32),
        "vals_words": valsp[0],
        "vals_scales": valsp[1],
        "dquery2": (n((D, Q)) * 1.0 / np.sqrt(D) * fd[:, None]).astype(np.float32),
        "base": (0.5 * n((Q, T))).astype(np.float32),
        "offs": striped(idx),
    }


def reference(query, query2, keys_words, keys_scales, strict, gout, vals_words, vals_scales, dquery2, base, offs):
    idx = unstriped(offs)
    keysu = unpack_weight(keys_words, keys_scales, "e2m1")
    valsu = unpack_weight(vals_words, vals_scales, "e2m1")
    queryq = mxq(f64(query), 0, "e4m3")
    keysidxg = keysu[:, idx]
    a = queryq.T @ keysidxg
    query2q = mxq(f64(query2), 0, "e4m3")
    b = query2q.T @ keysidxg
    dquery2q = mxq(f64(dquery2), 0, "e4m3")
    tb = dquery2q.T @ keysidxg
    s = a - softplus(b) * f64(strict)
    p = np.exp(s - np.max(s, axis=1, keepdims=True))
    z = np.sum(p, axis=1, keepdims=True)
    goutq = mxq(f64(gout), 0, "e4m3")
    valsidxg = valsu[:, idx]
    c0 = goutq.T @ valsidxg
    dz = np.sum(c0 * p / np.square(z) * (-1.0), axis=1, keepdims=True)
    dp = c0 / z + dz
    ds = dp * p
    ts = tb * sigmoid(b) * f64(strict) * (-1.0)
    tp = ts * p
    tz = np.sum(tp, axis=1, keepdims=True)
    tdz = np.sum((tp * c0 - tz * z * 2.0 * c0 * p / np.square(z)) / np.square(z) * (-1.0), axis=1, keepdims=True)
    tdp = tz * c0 / np.square(z) * (-1.0) + tdz
    tds = tdp * p + tp * dp
    tdb = tds * (-1.0) * f64(strict) * sigmoid(b) + tb * sigmoid(b) * (1.0 - sigmoid(b)) * ds * (-1.0) * f64(strict)
    gs = tdb * 512.0
    gf = np.zeros((Q, T))
    gf[:, idx] = gs
    y = f64(base) + gf
    return y

@@ -1,0 +1,185 @@
+from contextlib import ExitStack
+
+import concourse.mybir as mybir
+
+D, E, T, I, Q = 512, 512, 2048, 512, 128
+FLOPS = 4 * 2 * Q * I * D
+
+F32 = mybir.dt.float32
+BF16 = mybir.dt.bfloat16
+I32 = mybir.dt.int32
+U32 = mybir.dt.uint32
+U16 = mybir.dt.uint16
+U8 = mybir.dt.uint8
+FP8X4 = mybir.dt.float8_e4m3fn_x4
+FP4X4 = mybir.dt.float4_e2m1fn_x4
+ALU = mybir.AluOpType
+ACT = mybir.ActivationFunctionType
+
+P = 128
+PACK = 4
+HALF = I // 2
+STORE_WIDTHS = (256, 512, 512, 512, 256)
+LN_FLOOR = 2.0 ** -63
+
+
+def tile_attend_hvheldback_s_kernel(tc, query, query2, keys_words, keys_scales, strict, gout, vals_words, vals_scales, dquery2, base, offs, out):
+    nc = tc.nc
+    with ExitStack() as ctx:
+        sb = ctx.enter_context(tc.tile_pool(name="sb", bufs=1))
+        ps = ctx.enter_context(tc.psum_pool(name="ps", bufs=1))
+
+        def tile(name, shape, dtype):
+            return sb.tile(shape, dtype, name=name, align_bytes=64)
+
+        offsets = tile("offsets", [P, I // 16], U16)
+        kw = tile("kw", [P, T], U16)
+        ks = tile("ks", [P, T], U8)
+        vw = tile("vw", [P, T], U16)
+        vs = tile("vs", [P, T], U8)
+        floor = tile("floor", [P, 1], F32)
+        warm = tile("warm", [P, 1], F32)
+        window = tile("window", [P, T], F32)
+        res = tile("res", [P, T], F32)
+        k = tile("k", [P, 1], F32)
+
+        nc.vector.memset(ks[:].bitcast(I32), 0)
+        nc.vector.memset(floor[:], LN_FLOOR)
+        nc.vector.memset(vs[:].bitcast(I32), 0)
+        nc.vector.memset(window[:], 0.0)
+
+        def load_scales(engine, dst, src):
+            for quad in range(4):
+                engine.dma_start(out=dst[32 * quad : 32 * quad + 4, :].bitcast(I32), in_=src[0, 4 * quad : 4 * quad + 4, :].bitcast(I32))
+
+        raws = {}
+
+        def load_rows(name, src):
+            raw = tile("raw_" + name, [P, PACK, Q], F32)
+            nc.sync.dma_start(out=raw[:], in_=src.rearrange("(p j) q -> p j q", j=PACK))
+            raws[name] = raw
+
+        nc.sync.dma_start(offsets[:], offs)
+        nc.sync.dma_start(out=kw[:].bitcast(I32), in_=keys_words[0].bitcast(I32))
+        load_scales(nc.scalar, ks, keys_scales)
+        load_rows("q2", query2)
+        load_rows("dq2", dquery2)
+        load_rows("q", query)
+        load_rows("g", gout)
+        load_scales(nc.sync, vs, vals_scales)
+        nc.sync.dma_start(out=vw[:].bitcast(I32), in_=vals_words[0].bitcast(I32))
+        nc.sync.dma_start(out=k[:], in_=strict)
+        nc.sync.dma_start(out=res[:], in_=base)
+
+        nc.scalar.activation(out=warm[:], in_=floor[:], func=ACT.Sigmoid)
+
+        grouped = {}
+
+        def interleave(name):
+            g = tile("bf_" + name, [P, Q, PACK], BF16)
+            nc.scalar.copy(out=g[:].rearrange("p (c i) t -> p c t i", i=4), in_=raws[name][:].rearrange("p t (c i) -> p c t i", i=4))
+            grouped[name] = g
+
+        quant = {}
+
+        def quantise(name):
+            codes = tile("codes_" + name, [P, Q], U32)
+            scales = tile("scales_" + name, [P, Q], U8)
+            nc.vector.quantize_mx(out=codes[:].bitcast(FP8X4), scales=scales[:], in_=grouped[name][:].rearrange("p q t -> p (q t)"))
+            quant[name] = (codes, scales)
+
+        def scores(dst, name, words, scales, cols):
+            codes, qs = quant[name]
+            nc.tensor.matmul_mx(out=dst, lhsT=codes[:].bitcast(FP8X4), lhsT_scale=qs[:], rhs=words[:, cols].bitcast(FP4X4), rhs_scale=scales[:, cols], start=True, stop=True)
+
+        for name in ("q2", "dq2", "q", "g"):
+            interleave(name)
+
+        kwg = tile("kwg", [P, I], U16)
+        ksg = tile("ksg", [P, I], U8)
+        vwg = tile("vwg", [P, I], U16)
+        vsg = tile("vsg", [P, I], U8)
+        halves = [slice(h * HALF, (h + 1) * HALF) for h in range(2)]
+        lists = [offsets[:, h * (HALF // 16) : (h + 1) * (HALF // 16)] for h in range(2)]
+
+        nc.vector.tensor_copy(kwg[:], kw[:].indirect(offsets[:]))
+        quantise("q2")
+        b_ps = [ps.tile([P, HALF], F32, name="b%d" % h) for h in range(2)]
+        sig_n = tile("sig_n", [P, I], F32)
+        sig = tile("sig", [P, I], F32)
+        for h in range(2):
+            nc.vector.tensor_copy(ksg[:, halves[h]], ks[:].indirect(lists[h]))
+            scores(b_ps[h][:], "q2", kwg, ksg, halves[h])
+        for h in range(2):
+            nc.scalar.activation(out=sig_n[:, halves[h]], in_=b_ps[h][:], func=ACT.Sigmoid, scale=-1.0)
+            nc.scalar.activation(out=sig[:, halves[h]], in_=b_ps[h][:], func=ACT.Sigmoid)
+        everything = slice(0, I)
+        quantise("dq2")
+        tb_ps = ps.tile([P, I], F32, name="tb")
+        scores(tb_ps[:], "dq2", kwg, ksg, everything)
+        quantise("q")
+        a_ps = ps.tile([P, I], F32, name="a")
+        scores(a_ps[:], "q", kwg, ksg, everything)
+        quantise("g")
+        nc.vector.tensor_copy(vsg[:], vs[:].indirect(offsets[:]))
+        nc.vector.tensor_copy(vwg[:], vw[:].indirect(offsets[:]))
+        c_ps = ps.tile([P, I], F32, name="c")
+        scores(c_ps[:], "g", vwg, vsg, everything)
+
+        nk1 = tile("nk1", [P, 1], F32)
+        nc.gpsimd.tensor_scalar(out=nk1[:], in0=k[:], scalar1=-1.0, scalar2=-1.0, op0=ALU.mult, op1=ALU.add)
+        nk512 = tile("nk512", [P, 1], F32)
+        nc.gpsimd.tensor_scalar(out=nk512[:], in0=k[:], scalar1=-512.0, scalar2=0.0, op0=ALU.mult, op1=ALU.add)
+
+        u = tile("u", [P, I], F32)
+        nc.vector.tensor_tensor(out=u[:], in0=tb_ps[:], in1=sig[:], op=ALU.mult)
+
+        ln = tile("ln", [P, I], F32)
+        nsp = tile("nsp", [P, I], F32)
+        s = tile("s", [P, I], F32)
+        for h in range(2):
+            nc.scalar.activation(out=ln[:, halves[h]], in_=sig_n[:, halves[h]], func=ACT.Ln, bias=floor[:])
+        for h in range(2):
+            nc.vector.scalar_tensor_tensor(out=nsp[:, halves[h]], in0=b_ps[h][:], scalar=-1.0, in1=ln[:, halves[h]], op0=ALU.mult, op1=ALU.min)
+        for h in range(2):
+            nc.vector.scalar_tensor_tensor(out=s[:, halves[h]], in0=nsp[:, halves[h]], scalar=k[:], in1=a_ps[:, halves[h]], op0=ALU.mult, op1=ALU.add)
+        nmax = tile("nmax", [P, 1], F32)
+        nc.vector.tensor_reduce(out=nmax[:], in_=s[:], axis=mybir.AxisListType.X, op=ALU.max, negate=True)
+        p = tile("p", [P, I], F32)
+        z = tile("z", [P, 1], F32)
+        nc.scalar.activation(out=p[:], in_=s[:], func=ACT.Exp, bias=nmax[:], accum_out=z[:])
+        v = tile("v", [P, I], F32)
+        nc.vector.scalar_tensor_tensor(out=v[:], in0=u[:], scalar=nk1[:], in1=tb_ps[:], op0=ALU.mult, op1=ALU.add)
+
+        rz = tile("rz", [P, 1], F32)
+        nc.vector.reciprocal(out=rz[:], in_=z[:])
+        kpu = tile("kpu", [P, I], F32)
+        kpu_sum = tile("kpu_sum", [P, 1], F32)
+        nc.vector.scalar_tensor_tensor(out=kpu[:], in0=p[:], scalar=k[:], in1=u[:], op0=ALU.mult, op1=ALU.mult, accum_out=kpu_sum[:])
+        wc = tile("wc", [P, I], F32)
+        c_mean = tile("c_mean", [P, 1], F32)
+        nc.vector.scalar_tensor_tensor(out=wc[:], in0=p[:], scalar=rz[:], in1=c_ps[:], op0=ALU.mult, op1=ALU.mult, accum_out=c_mean[:])
+        gain = tile("gain", [P, 1], F32)
+        nc.vector.tensor_scalar(out=gain[:], in0=rz[:], scalar1=rz[:], scalar2=nk512[:], op0=ALU.mult, op1=ALU.mult)
+        psig = tile("psig", [P, I], F32)
+        nc.vector.tensor_tensor(out=psig[:], in0=p[:], in1=sig[:], op=ALU.mult)
+        f1 = tile("f1", [P, I], F32)
+        nc.scalar.activation(out=f1[:], in_=v[:], func=ACT.Identity, scale=z[:], bias=kpu_sum[:])
+        cov_terms = tile("cov_terms", [P, I], F32)
+        cov = tile("cov", [P, 1], F32)
+        nc.vector.scalar_tensor_tensor(out=cov_terms[:], in0=c_ps[:], scalar=c_mean[:], in1=kpu[:], op0=ALU.subtract, op1=ALU.mult, accum_out=cov[:])
+        f2 = tile("f2", [P, I], F32)
+        f3 = tile("f3", [P, I], F32)
+        for h in range(2):
+            nc.vector.scalar_tensor_tensor(out=f2[:, halves[h]], in0=c_ps[:, halves[h]], scalar=c_mean[:], in1=f1[:, halves[h]], op0=ALU.subtract, op1=ALU.mult)
+        for h in range(2):
+            nc.vector.tensor_scalar(out=f3[:, halves[h]], in0=f2[:, halves[h]], scalar1=cov[:], scalar2=gain[:], op0=ALU.add, op1=ALU.mult)
+        nc.vector.tensor_tensor(window[:].indirect(offsets[:]), f3[:], psig[:], ALU.mult)
+
+        start = 0
+        for n, width in enumerate(STORE_WIDTHS):
+            cols = slice(start, start + width)
+            nc.vector.tensor_tensor(out=res[:, cols], in0=res[:, cols], in1=window[:, cols], op=ALU.add)
+            queue = nc.sync if n % 2 == 0 else nc.scalar
+            queue.dma_start(out=out[:, cols], in_=res[:, cols])
+            start = start + width

@@ -19,7 +19,7 @@ ACT = mybir.ActivationFunctionType
 P = 128
 PACK = 4
 HALF = I // 2
-STORE_WIDTHS = (256, 512, 512, 512, 256)
+STORE_WIDTHS = (128, 512, 512, 512, 256, 128)
 LN_FLOOR = 2.0 ** -63
 
 
@@ -27,115 +27,116 @@ def tile_attend_hvheldback_s_kernel(tc, query, query2, keys_words, keys_scales, 
     nc = tc.nc
     with ExitStack() as ctx:
         sb = ctx.enter_context(tc.tile_pool(name="sb", bufs=1))
+        reuse = ctx.enter_context(tc.tile_pool(name="reuse", bufs=1))
         ps = ctx.enter_context(tc.psum_pool(name="ps", bufs=1))
 
-        def tile(name, shape, dtype):
-            return sb.tile(shape, dtype, name=name, align_bytes=64)
+        def tile(name, shape, dtype, after=None):
+            return sb.tile(shape, dtype, name=name, tag=after or name, align_bytes=64)
+
+        def placed(name, shape, dtype, offset):
+            return reuse.tile(shape, dtype, name=name, offset=offset, align_bytes=64)
 
         offsets = tile("offsets", [P, I // 16], U16)
-        kw = tile("kw", [P, T], U16)
         ks = tile("ks", [P, T], U8)
-        vw = tile("vw", [P, T], U16)
         vs = tile("vs", [P, T], U8)
         floor = tile("floor", [P, 1], F32)
-        warm = tile("warm", [P, 1], F32)
+        one = placed("one", [P, 3072], F32, 0)
+        warm = placed("warm", [P, 2560], F32, 12288)
         window = tile("window", [P, T], F32)
-        res = tile("res", [P, T], F32)
         k = tile("k", [P, 1], F32)
 
-        nc.vector.memset(ks[:].bitcast(I32), 0)
-        nc.vector.memset(floor[:], LN_FLOOR)
-        nc.vector.memset(vs[:].bitcast(I32), 0)
-        nc.vector.memset(window[:], 0.0)
+        nc.vector.memset(ks[:, : T // 2].bitcast(I32), 0)
+        nc.gpsimd.memset(ks[:, T // 2 :].bitcast(I32), 0)
+        nc.vector.memset(one[:, 0:1], 1.0)
+        nc.vector.tensor_scalar(out=floor[:], in0=one[:, 0:1], scalar1=LN_FLOOR, scalar2=None, op0=ALU.mult)
+        nc.gpsimd.memset(vs[:].bitcast(I32), 0)
+        nc.scalar.dma_start(out=k[:], in_=strict)
+        nc.gpsimd.memset(window[:], 0.0)
+        nc.scalar.activation(out=warm[:, 0:1], in_=floor[:], func=ACT.Sigmoid)
 
-        def load_scales(engine, dst, src):
+        def load_scales(dst, src):
             for quad in range(4):
-                engine.dma_start(out=dst[32 * quad : 32 * quad + 4, :].bitcast(I32), in_=src[0, 4 * quad : 4 * quad + 4, :].bitcast(I32))
+                nc.sync.dma_start(out=dst[32 * quad : 32 * quad + 4, :].bitcast(I32), in_=src[0, 4 * quad : 4 * quad + 4, :].bitcast(I32))
 
-        raws = {}
-
-        def load_rows(name, src):
-            raw = tile("raw_" + name, [P, PACK, Q], F32)
+        def load_rows(raw, src):
             nc.sync.dma_start(out=raw[:], in_=src.rearrange("(p j) q -> p j q", j=PACK))
-            raws[name] = raw
+            return raw
 
         nc.sync.dma_start(offsets[:], offs)
+        raw_q2 = load_rows(tile("raw_q2", [P, PACK, Q], F32), query2)
+        load_scales(ks, keys_scales)
+        kw = placed("kw", [P, T], U16, 0)
         nc.sync.dma_start(out=kw[:].bitcast(I32), in_=keys_words[0].bitcast(I32))
-        load_scales(nc.scalar, ks, keys_scales)
-        load_rows("q2", query2)
-        load_rows("dq2", dquery2)
-        load_rows("q", query)
-        load_rows("g", gout)
-        load_scales(nc.sync, vs, vals_scales)
+        raw_q = load_rows(placed("raw_q", [P, PACK, Q], F32, 4096), query)
+        raw_dq2 = load_rows(placed("raw_dq2", [P, PACK, Q], F32, 10240), dquery2)
+        vw = placed("vw", [P, T], U16, 6144)
         nc.sync.dma_start(out=vw[:].bitcast(I32), in_=vals_words[0].bitcast(I32))
-        nc.sync.dma_start(out=k[:], in_=strict)
+        load_scales(vs, vals_scales)
+        raw_g = load_rows(placed("raw_g", [P, PACK, Q], F32, 12288), gout)
+        res = placed("res", [P, T], F32, 14336)
         nc.sync.dma_start(out=res[:], in_=base)
 
-        nc.scalar.activation(out=warm[:], in_=floor[:], func=ACT.Sigmoid)
+        def interleave(copy, grouped, raw):
+            copy(out=grouped[:].rearrange("p (c i) t -> p c t i", i=4), in_=raw[:].rearrange("p t (c i) -> p c t i", i=4))
 
-        grouped = {}
-
-        def interleave(name):
-            g = tile("bf_" + name, [P, Q, PACK], BF16)
-            nc.scalar.copy(out=g[:].rearrange("p (c i) t -> p c t i", i=4), in_=raws[name][:].rearrange("p t (c i) -> p c t i", i=4))
-            grouped[name] = g
-
-        quant = {}
-
-        def quantise(name):
+        def quantise(name, grouped, scales):
             codes = tile("codes_" + name, [P, Q], U32)
-            scales = tile("scales_" + name, [P, Q], U8)
-            nc.vector.quantize_mx(out=codes[:].bitcast(FP8X4), scales=scales[:], in_=grouped[name][:].rearrange("p q t -> p (q t)"))
-            quant[name] = (codes, scales)
+            nc.vector.quantize_mx(out=codes[:].bitcast(FP8X4), scales=scales[:], in_=grouped[:].rearrange("p q t -> p (q t)"))
+            return codes, scales
 
-        def scores(dst, name, words, scales, cols):
-            codes, qs = quant[name]
-            nc.tensor.matmul_mx(out=dst, lhsT=codes[:].bitcast(FP8X4), lhsT_scale=qs[:], rhs=words[:, cols].bitcast(FP4X4), rhs_scale=scales[:, cols], start=True, stop=True)
+        def scores(dst, rows, words, scales, cols):
+            nc.tensor.matmul_mx(out=dst, lhsT=rows[0][:].bitcast(FP8X4), lhsT_scale=rows[1][:], rhs=words[:, cols].bitcast(FP4X4), rhs_scale=scales[:, cols], start=True, stop=True)
 
-        for name in ("q2", "dq2", "q", "g"):
-            interleave(name)
-
-        kwg = tile("kwg", [P, I], U16)
-        ksg = tile("ksg", [P, I], U8)
-        vwg = tile("vwg", [P, I], U16)
-        vsg = tile("vsg", [P, I], U8)
         halves = [slice(h * HALF, (h + 1) * HALF) for h in range(2)]
         lists = [offsets[:, h * (HALF // 16) : (h + 1) * (HALF // 16)] for h in range(2)]
+        everything = slice(0, I)
 
-        nc.vector.tensor_copy(kwg[:], kw[:].indirect(offsets[:]))
-        quantise("q2")
+        bf_q2 = tile("bf_q2", [P, Q, PACK], BF16)
+        interleave(nc.scalar.copy, bf_q2, raw_q2)
+        bf_q = tile("bf_q", [P, Q, PACK], BF16)
+        interleave(nc.scalar.copy, bf_q, raw_q)
+        bf_dq2 = placed("bf_dq2", [P, Q, PACK], BF16, 4096)
+        interleave(nc.scalar.copy, bf_dq2, raw_dq2)
+
+        kwg = tile("kwg", [P, I], U16, after="raw_q2")
+        ksg = tile("ksg", [P, I], U8)
+        nc.vector.tensor_copy(ksg[:], ks[:].indirect(offsets[:]))
+        mx_q2 = quantise("q2", bf_q2, tile("scales_q2", [P, Q], U8))
         b_ps = [ps.tile([P, HALF], F32, name="b%d" % h) for h in range(2)]
-        sig_n = tile("sig_n", [P, I], F32)
+        sig_n = placed("sig_n", [P, I], F32, 10240)
         sig = tile("sig", [P, I], F32)
         for h in range(2):
-            nc.vector.tensor_copy(ksg[:, halves[h]], ks[:].indirect(lists[h]))
-            scores(b_ps[h][:], "q2", kwg, ksg, halves[h])
+            nc.vector.tensor_copy(kwg[:, halves[h]], kw[:].indirect(lists[h]))
+            scores(b_ps[h][:], mx_q2, kwg, ksg, halves[h])
         for h in range(2):
             nc.scalar.activation(out=sig_n[:, halves[h]], in_=b_ps[h][:], func=ACT.Sigmoid, scale=-1.0)
             nc.scalar.activation(out=sig[:, halves[h]], in_=b_ps[h][:], func=ACT.Sigmoid)
-        everything = slice(0, I)
-        quantise("dq2")
-        tb_ps = ps.tile([P, I], F32, name="tb")
-        scores(tb_ps[:], "dq2", kwg, ksg, everything)
-        quantise("q")
+
+        mx_q = quantise("q", bf_q, placed("scales_q", [P, Q], U8, 3584))
         a_ps = ps.tile([P, I], F32, name="a")
-        scores(a_ps[:], "q", kwg, ksg, everything)
-        quantise("g")
-        nc.vector.tensor_copy(vsg[:], vs[:].indirect(offsets[:]))
+        scores(a_ps[:], mx_q, kwg, ksg, everything)
+        mx_dq2 = quantise("dq2", bf_dq2, placed("scales_dq2", [P, Q], U8, 3712))
+        tb_ps = ps.tile([P, I], F32, name="tb")
+        scores(tb_ps[:], mx_dq2, kwg, ksg, everything)
+        vwg = placed("vwg", [P, I], U16, 0)
+        vsg = placed("vsg", [P, I], U8, 1024)
         nc.vector.tensor_copy(vwg[:], vw[:].indirect(offsets[:]))
+        nc.vector.tensor_copy(vsg[:], vs[:].indirect(offsets[:]))
+        bf_g = placed("bf_g", [P, Q, PACK], BF16, 2560)
+        interleave(nc.vector.tensor_copy, bf_g, raw_g)
+        mx_g = quantise("g", bf_g, tile("scales_g", [P, Q], U8))
         c_ps = ps.tile([P, I], F32, name="c")
-        scores(c_ps[:], "g", vwg, vsg, everything)
+        scores(c_ps[:], mx_g, vwg, vsg, everything)
 
         nk1 = tile("nk1", [P, 1], F32)
         nc.gpsimd.tensor_scalar(out=nk1[:], in0=k[:], scalar1=-1.0, scalar2=-1.0, op0=ALU.mult, op1=ALU.add)
         nk512 = tile("nk512", [P, 1], F32)
         nc.gpsimd.tensor_scalar(out=nk512[:], in0=k[:], scalar1=-512.0, scalar2=0.0, op0=ALU.mult, op1=ALU.add)
-
-        u = tile("u", [P, I], F32)
-        nc.vector.tensor_tensor(out=u[:], in0=tb_ps[:], in1=sig[:], op=ALU.mult)
+        slope = tile("slope", [P, I], F32)
+        nc.gpsimd.tensor_scalar(out=slope[:], in0=sig[:], scalar1=nk1[:], scalar2=1.0, op0=ALU.mult, op1=ALU.add)
 
         ln = tile("ln", [P, I], F32)
-        nsp = tile("nsp", [P, I], F32)
+        nsp = placed("nsp", [P, I], F32, 1536)
         s = tile("s", [P, I], F32)
         for h in range(2):
             nc.scalar.activation(out=ln[:, halves[h]], in_=sig_n[:, halves[h]], func=ACT.Ln, bias=floor[:])
@@ -148,21 +149,23 @@ def tile_attend_hvheldback_s_kernel(tc, query, query2, keys_words, keys_scales, 
         p = tile("p", [P, I], F32)
         z = tile("z", [P, 1], F32)
         nc.scalar.activation(out=p[:], in_=s[:], func=ACT.Exp, bias=nmax[:], accum_out=z[:])
-        v = tile("v", [P, I], F32)
-        nc.vector.scalar_tensor_tensor(out=v[:], in0=u[:], scalar=nk1[:], in1=tb_ps[:], op0=ALU.mult, op1=ALU.add)
+        v = placed("v", [P, I], F32, 1536)
+        nc.vector.tensor_tensor(out=v[:], in0=tb_ps[:], in1=slope[:], op=ALU.mult)
 
         rz = tile("rz", [P, 1], F32)
         nc.vector.reciprocal(out=rz[:], in_=z[:])
-        kpu = tile("kpu", [P, I], F32)
-        kpu_sum = tile("kpu_sum", [P, 1], F32)
-        nc.vector.scalar_tensor_tensor(out=kpu[:], in0=p[:], scalar=k[:], in1=u[:], op0=ALU.mult, op1=ALU.mult, accum_out=kpu_sum[:])
+        psig = tile("psig", [P, I], F32)
+        nc.vector.tensor_tensor(out=psig[:], in0=p[:], in1=sig[:], op=ALU.mult)
         wc = tile("wc", [P, I], F32)
         c_mean = tile("c_mean", [P, 1], F32)
         nc.vector.scalar_tensor_tensor(out=wc[:], in0=p[:], scalar=rz[:], in1=c_ps[:], op0=ALU.mult, op1=ALU.mult, accum_out=c_mean[:])
+        kpu = tile("kpu", [P, I], F32)
+        kpu_sum = tile("kpu_sum", [P, 1], F32)
+        nc.vector.scalar_tensor_tensor(out=kpu[:], in0=psig[:], scalar=k[:], in1=tb_ps[:], op0=ALU.mult, op1=ALU.mult, accum_out=kpu_sum[:])
         gain = tile("gain", [P, 1], F32)
-        nc.vector.tensor_scalar(out=gain[:], in0=rz[:], scalar1=rz[:], scalar2=nk512[:], op0=ALU.mult, op1=ALU.mult)
-        psig = tile("psig", [P, I], F32)
-        nc.vector.tensor_tensor(out=psig[:], in0=p[:], in1=sig[:], op=ALU.mult)
+        gain_z = tile("gain_z", [P, 1], F32)
+        nc.scalar.activation(out=gain_z[:], in_=rz[:], func=ACT.Identity, scale=nk512[:])
+        nc.scalar.activation(out=gain[:], in_=gain_z[:], func=ACT.Identity, scale=rz[:])
         f1 = tile("f1", [P, I], F32)
         nc.scalar.activation(out=f1[:], in_=v[:], func=ACT.Identity, scale=z[:], bias=kpu_sum[:])
         cov_terms = tile("cov_terms", [P, I], F32)

@@ -19,7 +19,7 @@ ACT = mybir.ActivationFunctionType
 P = 128
 PACK = 4
 HALF = I // 2
-STORE_WIDTHS = (128, 512, 512, 512, 256, 128)
+STORE_WIDTHS = (256, 512, 512, 512, 256)
 LN_FLOOR = 2.0 ** -63
 
 
@@ -45,13 +45,12 @@ def tile_attend_hvheldback_s_kernel(tc, query, query2, keys_words, keys_scales, 
         window = tile("window", [P, T], F32)
         k = tile("k", [P, 1], F32)
 
-        nc.vector.memset(ks[:, : T // 2].bitcast(I32), 0)
-        nc.gpsimd.memset(ks[:, T // 2 :].bitcast(I32), 0)
+        nc.vector.memset(ks[:].bitcast(I32), 0)
         nc.vector.memset(one[:, 0:1], 1.0)
         nc.vector.tensor_scalar(out=floor[:], in0=one[:, 0:1], scalar1=LN_FLOOR, scalar2=None, op0=ALU.mult)
-        nc.gpsimd.memset(vs[:].bitcast(I32), 0)
+        nc.vector.memset(vs[:].bitcast(I32), 0)
         nc.scalar.dma_start(out=k[:], in_=strict)
-        nc.gpsimd.memset(window[:], 0.0)
+        nc.vector.memset(window[:], 0.0)
         nc.scalar.activation(out=warm[:, 0:1], in_=floor[:], func=ACT.Sigmoid)
 
         def load_scales(dst, src):
@@ -129,11 +128,11 @@ def tile_attend_hvheldback_s_kernel(tc, query, query2, keys_words, keys_scales, 
         scores(c_ps[:], mx_g, vwg, vsg, everything)
 
         nk1 = tile("nk1", [P, 1], F32)
-        nc.gpsimd.tensor_scalar(out=nk1[:], in0=k[:], scalar1=-1.0, scalar2=-1.0, op0=ALU.mult, op1=ALU.add)
+        nc.vector.tensor_scalar(out=nk1[:], in0=k[:], scalar1=-1.0, scalar2=-1.0, op0=ALU.mult, op1=ALU.add)
         nk512 = tile("nk512", [P, 1], F32)
-        nc.gpsimd.tensor_scalar(out=nk512[:], in0=k[:], scalar1=-512.0, scalar2=0.0, op0=ALU.mult, op1=ALU.add)
-        slope = tile("slope", [P, I], F32)
-        nc.gpsimd.tensor_scalar(out=slope[:], in0=sig[:], scalar1=nk1[:], scalar2=1.0, op0=ALU.mult, op1=ALU.add)
+        nc.vector.tensor_scalar(out=nk512[:], in0=k[:], scalar1=-512.0, scalar2=None, op0=ALU.mult)
+        u = tile("u", [P, I], F32)
+        nc.vector.tensor_tensor(out=u[:], in0=tb_ps[:], in1=sig[:], op=ALU.mult)
 
         ln = tile("ln", [P, I], F32)
         nsp = placed("nsp", [P, I], F32, 1536)
@@ -150,18 +149,18 @@ def tile_attend_hvheldback_s_kernel(tc, query, query2, keys_words, keys_scales, 
         z = tile("z", [P, 1], F32)
         nc.scalar.activation(out=p[:], in_=s[:], func=ACT.Exp, bias=nmax[:], accum_out=z[:])
         v = placed("v", [P, I], F32, 1536)
-        nc.vector.tensor_tensor(out=v[:], in0=tb_ps[:], in1=slope[:], op=ALU.mult)
+        nc.vector.scalar_tensor_tensor(out=v[:], in0=u[:], scalar=nk1[:], in1=tb_ps[:], op0=ALU.mult, op1=ALU.add)
 
         rz = tile("rz", [P, 1], F32)
         nc.vector.reciprocal(out=rz[:], in_=z[:])
-        psig = tile("psig", [P, I], F32)
-        nc.vector.tensor_tensor(out=psig[:], in0=p[:], in1=sig[:], op=ALU.mult)
+        kpu = tile("kpu", [P, I], F32)
+        kpu_sum = tile("kpu_sum", [P, 1], F32)
+        nc.vector.scalar_tensor_tensor(out=kpu[:], in0=p[:], scalar=k[:], in1=u[:], op0=ALU.mult, op1=ALU.mult, accum_out=kpu_sum[:])
         wc = tile("wc", [P, I], F32)
         c_mean = tile("c_mean", [P, 1], F32)
         nc.vector.scalar_tensor_tensor(out=wc[:], in0=p[:], scalar=rz[:], in1=c_ps[:], op0=ALU.mult, op1=ALU.mult, accum_out=c_mean[:])
-        kpu = tile("kpu", [P, I], F32)
-        kpu_sum = tile("kpu_sum", [P, 1], F32)
-        nc.vector.scalar_tensor_tensor(out=kpu[:], in0=psig[:], scalar=k[:], in1=tb_ps[:], op0=ALU.mult, op1=ALU.mult, accum_out=kpu_sum[:])
+        psig = tile("psig", [P, I], F32)
+        nc.vector.tensor_tensor(out=psig[:], in0=p[:], in1=sig[:], op=ALU.mult)
         gain = tile("gain", [P, 1], F32)
         gain_z = tile("gain_z", [P, 1], F32)
         nc.scalar.activation(out=gain_z[:], in_=rz[:], func=ACT.Identity, scale=nk512[:])

from contextlib import ExitStack

import concourse.mybir as mybir

D, E, T, I, Q = 512, 512, 2048, 512, 128
FLOPS = 4 * 2 * Q * I * D

F32 = mybir.dt.float32
BF16 = mybir.dt.bfloat16
I32 = mybir.dt.int32
U32 = mybir.dt.uint32
U16 = mybir.dt.uint16
U8 = mybir.dt.uint8
FP8X4 = mybir.dt.float8_e4m3fn_x4
FP4X4 = mybir.dt.float4_e2m1fn_x4
ALU = mybir.AluOpType
ACT = mybir.ActivationFunctionType

P = 128
PACK = 4
HALF = I // 2
STORE_WIDTHS = (256, 512, 512, 512, 256)
LN_FLOOR = 2.0 ** -63


def tile_attend_hvheldback_s_kernel(tc, query, query2, keys_words, keys_scales, strict, gout, vals_words, vals_scales, dquery2, base, offs, out):
    nc = tc.nc
    with ExitStack() as ctx:
        sb = ctx.enter_context(tc.tile_pool(name="sb", bufs=1))
        reuse = ctx.enter_context(tc.tile_pool(name="reuse", bufs=1))
        ps = ctx.enter_context(tc.psum_pool(name="ps", bufs=1))

        def tile(name, shape, dtype, after=None):
            return sb.tile(shape, dtype, name=name, tag=after or name, align_bytes=64)

        def placed(name, shape, dtype, offset):
            return reuse.tile(shape, dtype, name=name, offset=offset, align_bytes=64)

        offsets = tile("offsets", [P, I // 16], U16)
        ks = tile("ks", [P, T], U8)
        vs = tile("vs", [P, T], U8)
        floor = tile("floor", [P, 1], F32)
        one = placed("one", [P, 3072], F32, 0)
        warm = placed("warm", [P, 2560], F32, 12288)
        window = tile("window", [P, T], F32)
        k = tile("k", [P, 1], F32)

        nc.vector.memset(ks[:].bitcast(I32), 0)
        nc.vector.memset(one[:, 0:1], 1.0)
        nc.vector.tensor_scalar(out=floor[:], in0=one[:, 0:1], scalar1=LN_FLOOR, scalar2=None, op0=ALU.mult)
        nc.vector.memset(vs[:].bitcast(I32), 0)
        nc.scalar.dma_start(out=k[:], in_=strict)
        nc.vector.memset(window[:], 0.0)
        nc.scalar.activation(out=warm[:, 0:1], in_=floor[:], func=ACT.Sigmoid)

        def load_scales(dst, src):
            for quad in range(4):
                nc.sync.dma_start(out=dst[32 * quad : 32 * quad + 4, :].bitcast(I32), in_=src[0, 4 * quad : 4 * quad + 4, :].bitcast(I32))

        def load_rows(raw, src):
            nc.sync.dma_start(out=raw[:], in_=src.rearrange("(p j) q -> p j q", j=PACK))
            return raw

        nc.sync.dma_start(offsets[:], offs)
        raw_q2 = load_rows(tile("raw_q2", [P, PACK, Q], F32), query2)
        load_scales(ks, keys_scales)
        kw = placed("kw", [P, T], U16, 0)
        nc.sync.dma_start(out=kw[:].bitcast(I32), in_=keys_words[0].bitcast(I32))
        raw_q = load_rows(placed("raw_q", [P, PACK, Q], F32, 4096), query)
        raw_dq2 = load_rows(placed("raw_dq2", [P, PACK, Q], F32, 10240), dquery2)
        vw = placed("vw", [P, T], U16, 6144)
        nc.sync.dma_start(out=vw[:].bitcast(I32), in_=vals_words[0].bitcast(I32))
        load_scales(vs, vals_scales)
        raw_g = load_rows(placed("raw_g", [P, PACK, Q], F32, 12288), gout)
        res = placed("res", [P, T], F32, 14336)
        nc.sync.dma_start(out=res[:], in_=base)

        def interleave(copy, grouped, raw):
            copy(out=grouped[:].rearrange("p (c i) t -> p c t i", i=4), in_=raw[:].rearrange("p t (c i) -> p c t i", i=4))

        def quantise(name, grouped, scales):
            codes = tile("codes_" + name, [P, Q], U32)
            nc.vector.quantize_mx(out=codes[:].bitcast(FP8X4), scales=scales[:], in_=grouped[:].rearrange("p q t -> p (q t)"))
            return codes, scales

        def scores(dst, rows, words, scales, cols):
            nc.tensor.matmul_mx(out=dst, lhsT=rows[0][:].bitcast(FP8X4), lhsT_scale=rows[1][:], rhs=words[:, cols].bitcast(FP4X4), rhs_scale=scales[:, cols], start=True, stop=True)

        halves = [slice(h * HALF, (h + 1) * HALF) for h in range(2)]
        lists = [offsets[:, h * (HALF // 16) : (h + 1) * (HALF // 16)] for h in range(2)]
        everything = slice(0, I)

        bf_q2 = tile("bf_q2", [P, Q, PACK], BF16)
        interleave(nc.scalar.copy, bf_q2, raw_q2)
        bf_q = tile("bf_q", [P, Q, PACK], BF16)
        interleave(nc.scalar.copy, bf_q, raw_q)
        bf_dq2 = placed("bf_dq2", [P, Q, PACK], BF16, 4096)
        interleave(nc.scalar.copy, bf_dq2, raw_dq2)

        kwg = tile("kwg", [P, I], U16, after="raw_q2")
        ksg = tile("ksg", [P, I], U8)
        nc.vector.tensor_copy(ksg[:], ks[:].indirect(offsets[:]))
        mx_q2 = quantise("q2", bf_q2, tile("scales_q2", [P, Q], U8))
        b_ps = [ps.tile([P, HALF], F32, name="b%d" % h) for h in range(2)]
        sig_n = placed("sig_n", [P, I], F32, 10240)
        sig = tile("sig", [P, I], F32)
        for h in range(2):
            nc.vector.tensor_copy(kwg[:, halves[h]], kw[:].indirect(lists[h]))
            scores(b_ps[h][:], mx_q2, kwg, ksg, halves[h])
        for h in range(2):
            nc.scalar.activation(out=sig_n[:, halves[h]], in_=b_ps[h][:], func=ACT.Sigmoid, scale=-1.0)
            nc.scalar.activation(out=sig[:, halves[h]], in_=b_ps[h][:], func=ACT.Sigmoid)

        mx_q = quantise("q", bf_q, placed("scales_q", [P, Q], U8, 3584))
        a_ps = ps.tile([P, I], F32, name="a")
        scores(a_ps[:], mx_q, kwg, ksg, everything)
        mx_dq2 = quantise("dq2", bf_dq2, placed("scales_dq2", [P, Q], U8, 3712))
        tb_ps = ps.tile([P, I], F32, name="tb")
        scores(tb_ps[:], mx_dq2, kwg, ksg, everything)
        vwg = placed("vwg", [P, I], U16, 0)
        vsg = placed("vsg", [P, I], U8, 1024)
        nc.vector.tensor_copy(vwg[:], vw[:].indirect(offsets[:]))
        nc.vector.tensor_copy(vsg[:], vs[:].indirect(offsets[:]))
        bf_g = placed("bf_g", [P, Q, PACK], BF16, 2560)
        interleave(nc.vector.tensor_copy, bf_g, raw_g)
        mx_g = quantise("g", bf_g, tile("scales_g", [P, Q], U8))
        c_ps = ps.tile([P, I], F32, name="c")
        scores(c_ps[:], mx_g, vwg, vsg, everything)

        nk1 = tile("nk1", [P, 1], F32)
        nc.vector.tensor_scalar(out=nk1[:], in0=k[:], scalar1=-1.0, scalar2=-1.0, op0=ALU.mult, op1=ALU.add)
        nk512 = tile("nk512", [P, 1], F32)
        nc.vector.tensor_scalar(out=nk512[:], in0=k[:], scalar1=-512.0, scalar2=None, op0=ALU.mult)
        u = tile("u", [P, I], F32)
        nc.vector.tensor_tensor(out=u[:], in0=tb_ps[:], in1=sig[:], op=ALU.mult)

        ln = tile("ln", [P, I], F32)
        nsp = placed("nsp", [P, I], F32, 1536)
        s = tile("s", [P, I], F32)
        for h in range(2):
            nc.scalar.activation(out=ln[:, halves[h]], in_=sig_n[:, halves[h]], func=ACT.Ln, bias=floor[:])
        for h in range(2):
            nc.vector.scalar_tensor_tensor(out=nsp[:, halves[h]], in0=b_ps[h][:], scalar=-1.0, in1=ln[:, halves[h]], op0=ALU.mult, op1=ALU.min)
        for h in range(2):
            nc.vector.scalar_tensor_tensor(out=s[:, halves[h]], in0=nsp[:, halves[h]], scalar=k[:], in1=a_ps[:, halves[h]], op0=ALU.mult, op1=ALU.add)
        nmax = tile("nmax", [P, 1], F32)
        nc.vector.tensor_reduce(out=nmax[:], in_=s[:], axis=mybir.AxisListType.X, op=ALU.max, negate=True)
        p = tile("p", [P, I], F32)
        z = tile("z", [P, 1], F32)
        nc.scalar.activation(out=p[:], in_=s[:], func=ACT.Exp, bias=nmax[:], accum_out=z[:])
        v = placed("v", [P, I], F32, 1536)
        nc.vector.scalar_tensor_tensor(out=v[:], in0=u[:], scalar=nk1[:], in1=tb_ps[:], op0=ALU.mult, op1=ALU.add)

        rz = tile("rz", [P, 1], F32)
        nc.vector.reciprocal(out=rz[:], in_=z[:])
        kpu = tile("kpu", [P, I], F32)
        kpu_sum = tile("kpu_sum", [P, 1], F32)
        nc.vector.scalar_tensor_tensor(out=kpu[:], in0=p[:], scalar=k[:], in1=u[:], op0=ALU.mult, op1=ALU.mult, accum_out=kpu_sum[:])
        wc = tile("wc", [P, I], F32)
        c_mean = tile("c_mean", [P, 1], F32)
        nc.vector.scalar_tensor_tensor(out=wc[:], in0=p[:], scalar=rz[:], in1=c_ps[:], op0=ALU.mult, op1=ALU.mult, accum_out=c_mean[:])
        psig = tile("psig", [P, I], F32)
        nc.vector.tensor_tensor(out=psig[:], in0=p[:], in1=sig[:], op=ALU.mult)
        gain = tile("gain", [P, 1], F32)
        gain_z = tile("gain_z", [P, 1], F32)
        nc.scalar.activation(out=gain_z[:], in_=rz[:], func=ACT.Identity, scale=nk512[:])
        nc.scalar.activation(out=gain[:], in_=gain_z[:], func=ACT.Identity, scale=rz[:])
        f1 = tile("f1", [P, I], F32)
        nc.scalar.activation(out=f1[:], in_=v[:], func=ACT.Identity, scale=z[:], bias=kpu_sum[:])
        cov_terms = tile("cov_terms", [P, I], F32)
        cov = tile("cov", [P, 1], F32)
        nc.vector.scalar_tensor_tensor(out=cov_terms[:], in0=c_ps[:], scalar=c_mean[:], in1=kpu[:], op0=ALU.subtract, op1=ALU.mult, accum_out=cov[:])
        f2 = tile("f2", [P, I], F32)
        f3 = tile("f3", [P, I], F32)
        for h in range(2):
            nc.vector.scalar_tensor_tensor(out=f2[:, halves[h]], in0=c_ps[:, halves[h]], scalar=c_mean[:], in1=f1[:, halves[h]], op0=ALU.subtract, op1=ALU.mult)
        for h in range(2):
            nc.vector.tensor_scalar(out=f3[:, halves[h]], in0=f2[:, halves[h]], scalar1=cov[:], scalar2=gain[:], op0=ALU.add, op1=ALU.mult)
        nc.vector.tensor_tensor(window[:].indirect(offsets[:]), f3[:], psig[:], ALU.mult)

        start = 0
        for n, width in enumerate(STORE_WIDTHS):
            cols = slice(start, start + width)
            nc.vector.tensor_tensor(out=res[:, cols], in0=res[:, cols], in1=window[:, cols], op=ALU.add)
            queue = nc.sync if n % 2 == 0 else nc.scalar
            queue.dma_start(out=out[:, cols], in_=res[:, cols])
            start = start + width
